import numpy as np
import ml_dtypes


def mxq(x, axis, fmt="e4m3"):
    dtype, down = {"e4m3": (ml_dtypes.float8_e4m3fn, 7), "e5m2": (ml_dtypes.float8_e5m2, 14)}[fmt]
    v = np.moveaxis(np.asarray(x, np.float32).astype(ml_dtypes.bfloat16).astype(np.float64), axis, -1)
    blocks = v.reshape(v.shape[:-1] + (-1, 32))
    amax = np.abs(blocks).max(-1, keepdims=True)
    byte = np.maximum(np.where(amax > 0, np.frexp(amax)[1] - 1 + 127, 0) - down, 1)
    scale = np.exp2(byte - 127.0)
    codes = (blocks / scale).astype(np.float32).astype(dtype).astype(np.float64)
    return np.moveaxis((codes * scale).reshape(v.shape), -1, axis)


WIDE = False


def mx_kscale(k):
    if not WIDE:
        return np.ones(k)
    levels = np.array([10, -10, 5, -5, 0])
    if k % 512:
        return np.exp2(np.random.permutation(np.resize(levels, k // 32))).repeat(32)
    a = np.empty((k // 512, 16))
    for p in range(k // 512):
        a[p, :8] = np.random.permutation(np.resize(levels, 8))
        for g in range(8):
            far = levels[np.abs(levels - a[p, g]) >= 10]
            a[p, g + 8] = far[np.random.randint(len(far))]
    return np.exp2(a.ravel()).repeat(32)


def f64(x):
    return np.asarray(x).astype(np.float64)


def striped(idx):
    return np.tile(np.asarray(idx).reshape(-1, 16).T, (8, 1)).astype(np.uint16)


def unstriped(offs):
    return offs[:16].T.reshape(-1).astype(np.int64)


E2M1 = np.array([0.0, 0.5, 1.0, 1.5, 2.0, 3.0, 4.0, 6.0, -0.0, -0.5, -1.0, -1.5, -2.0, -3.0, -4.0, -6.0])


def pack_weight(w, fmt):
    k, n = w.shape
    w = f64(np.asarray(w, np.float32).astype(ml_dtypes.bfloat16)).reshape(k // 32, 32, n)
    amax = np.abs(w).max(1)
    if fmt == "e4m3":
        byte = np.frexp(amax)[1] - 1 + 127 - 7
    else:
        mant, ex = np.frexp(amax / 6.0)
        byte = np.where(mant > 0.5, ex, ex - 1) + 127
    byte = np.clip(np.where(amax > 0, byte, 1), 1, 254)
    scaled = (w * np.exp2(127.0 - byte)[:, None, :]).reshape(k, n).astype(np.float32)
    by_word = np.ascontiguousarray(scaled.reshape(k // 512, 128, 4, n).transpose(0, 1, 3, 2))
    if fmt == "e4m3":
        words = by_word.astype(ml_dtypes.float8_e4m3fn).view(np.uint8)
    else:
        c = by_word.astype(ml_dtypes.float4_e2m1fn).view(np.uint8) & 0xF
        words = (c[..., 0::2] | (c[..., 1::2] << 4)).reshape(k // 512, 128, 2 * n)
    return np.ascontiguousarray(words), np.ascontiguousarray(byte.astype(np.uint8).reshape(k // 512, 16, n))


def unpack_weight(words, scales, fmt):
    g, _, n = scales.shape
    words = np.ascontiguousarray(words).reshape(g, 128, n, -1)
    if fmt == "e4m3":
        vals = words.view(ml_dtypes.float8_e4m3fn).astype(np.float64)
    else:
        nib = np.empty((g, 128, n, 4), np.uint8)
        nib[..., 0::2] = words & 0xF
        nib[..., 1::2] = words >> 4
        vals = E2M1[nib]
    vals = vals * np.repeat(np.exp2(scales.astype(np.float64) - 127.0), 8, axis=1)[..., None]
    return vals.transpose(0, 1, 3, 2).reshape(g * 512, n)


def sigmoid(v):
    return 1.0 / (1.0 + np.exp(-v))


D, E, T, I, Q, G = 512, 512, 2048, 512, 128, 32


def setup_inputs():
    n = np.random.standard_normal
    idx = np.random.permutation(T)[:I]
    fd = mx_kscale(D)
    fe = mx_kscale(E)
    keysp = pack_weight(n((D, T)) / fd[:, None], "e4m3")
    valsp = pack_weight(n((E, T)) / fe[:, None], "e4m3")
    return {
        "query": (n((D, Q)) * 0.5 / np.sqrt(D) * fd[:, None]).astype(np.float32),
        "keys_words": keysp[0],
        "keys_scales": keysp[1],
        "helpf": (np.random.uniform(0.5, 1.5, (Q, 1))).astype(np.float32),
        "gout": (n((E, Q)) * 1 / np.sqrt(E) * fe[:, None]).astype(np.float32),
        "vals_words": valsp[0],
        "vals_scales": valsp[1],
        "dquery": (n((D, Q)) * 1.0 / np.sqrt(D) * fd[:, None]).astype(np.float32),
        "base": (0.5 * n((Q, T))).astype(np.float32),
        "offs": striped(idx),
    }


def reference(query, keys_words, keys_scales, helpf, gout, vals_words, vals_scales, dquery, base, offs):
    idx = unstriped(offs)
    keysu = unpack_weight(keys_words, keys_scales, "e4m3")
    valsu = unpack_weight(vals_words, vals_scales, "e4m3")
    queryq = mxq(f64(query), 0, "e4m3")
    keysidxg = keysu[:, idx]
    a = queryq.T @ keysidxg
    dqueryq = mxq(f64(dquery), 0, "e4m3")
    ta = dqueryq.T @ keysidxg
    m1 = a.reshape(Q, G, I // G).mean(axis=2)
    gt = sigmoid(m1 * 4.0)
    gr = np.repeat(gt, I // G, axis=1)
    s = a * (gr * f64(helpf) + 1.0)
    p = np.exp(s - np.max(s, axis=1, keepdims=True))
    z = np.sum(p, axis=1, keepdims=True)
    goutq = mxq(f64(gout), 0, "e4m3")
    valsidxg = valsu[:, idx]
    c0 = goutq.T @ valsidxg
    dz = np.sum(c0 * p / np.square(z) * (-1.0), axis=1, keepdims=True)
    dp = c0 / z + dz
    ds = dp * p
    dgr = ds * a * f64(helpf)
    dgt = dgr.reshape(Q, G, I // G).sum(axis=2)
    tm1 = ta.reshape(Q, G, I // G).mean(axis=2)
    tgt = tm1 * 4.0 * gt * (1.0 - gt)
    tgr = np.repeat(tgt, I // G, axis=1)
    ts = ta * (gr * f64(helpf) + 1.0) + tgr * f64(helpf) * a
    tp = ts * p
    tz = np.sum(tp, axis=1, keepdims=True)
    tdz = np.sum((tp * c0 - tz * z * 2.0 * c0 * p / np.square(z)) / np.square(z) * (-1.0), axis=1, keepdims=True)
    tdp = tz * c0 / np.square(z) * (-1.0) + tdz
    tds = tdp * p + tp * dp
    tdgr = (tds * a + ta * ds) * f64(helpf)
    tdgt = tdgr.reshape(Q, G, I // G).sum(axis=2)
    tdm1 = ((tdgt * gt + tgt * dgt) * (1.0 - gt) + tgt * (-1.0) * dgt * gt) * 4.0
    te1 = tdm1 / 16.0
    tr1 = np.repeat(te1, I // G, axis=1)
    tda = tds * (gr * f64(helpf) + 1.0) + tgr * f64(helpf) * ds + tr1
    gs = tda * 512.0
    gf = np.zeros((Q, T))
    gf[:, idx] = gs
    y = f64(base) + gf
    return y

@@ -1,0 +1,200 @@
+from contextlib import ExitStack
+
+import concourse.mybir as mybir
+
+D, E, T, I, Q, G = 512, 512, 2048, 512, 128, 32
+FLOPS = 3 * 2 * 512 * 512 * 128
+
+F32 = mybir.dt.float32
+BF16 = mybir.dt.bfloat16
+I32 = mybir.dt.int32
+U32 = mybir.dt.uint32
+U16 = mybir.dt.uint16
+U8 = mybir.dt.uint8
+FP8X4 = mybir.dt.float8_e4m3fn_x4
+ALU = mybir.AluOpType
+ACT = mybir.ActivationFunctionType
+AX = mybir.AxisListType
+
+P = 128
+PACK = 4
+PAGE = I // G
+V_ROW = 4
+CHUNKS = 4
+
+
+def tile_attend_hvpagemates_s_kernel(tc, query, keys_words, keys_scales, helpf, gout, vals_words, vals_scales, dquery, base, offs, out):
+    nc = tc.nc
+    with ExitStack() as ctx:
+        sb = ctx.enter_context(tc.tile_pool(name="sb", bufs=1))
+        ps = ctx.enter_context(tc.psum_pool(name="ps", bufs=1))
+
+        def wide(name):
+            return sb.tile([P, I], F32, name=name, align_bytes=64)
+
+        def col(name, n=1):
+            return sb.tile([P, n], F32, name=name)
+
+        def paged(ap):
+            return ap.rearrange("p (g j) -> p g j", j=PAGE)
+
+        def spread(ap):
+            return ap.unsqueeze(2).to_broadcast([P, G, PAGE])
+
+        def by_page(dst, src, factor):
+            for g in range(G):
+                cols = slice(g * PAGE, (g + 1) * PAGE)
+                nc.scalar.activation(dst[:, cols], src[:, cols], ACT.Copy, scale=factor[:, g : g + 1])
+
+        offsets = sb.tile([P, I // 16], U16, name="offsets")
+        k_words = sb.tile([P, T], U32, name="k_words", align_bytes=64)
+        v_words = sb.tile([P, T], U32, name="v_words", align_bytes=64)
+        k_bytes = sb.tile([P, T], U8, name="k_bytes", align_bytes=64)
+        v_bytes = sb.tile([P, T], U8, name="v_bytes", align_bytes=64)
+        window = sb.tile([P, T], F32, name="window", align_bytes=64)
+        h = col("h")
+
+        nc.vector.memset(k_bytes[:].bitcast(I32), 0)
+        nc.vector.memset(v_bytes[:].bitcast(I32), 0)
+        nc.vector.memset(window[:], 0.0)
+
+        def load_words(dst, src):
+            nc.sync.dma_start(dst[:].bitcast(I32), src[0].rearrange("p n t -> p (n t)").bitcast(I32))
+
+        def load_bytes(queue, dst, src, row):
+            for quad in range(4):
+                queue.dma_start(dst[32 * quad + row : 32 * quad + row + 4, :].bitcast(I32), src[0, 4 * quad : 4 * quad + 4, :].bitcast(I32))
+
+        def load_rows(name, src, tag):
+            raw = sb.tile([P, PACK, Q], F32, name=name, tag=tag, align_bytes=64)
+            nc.sync.dma_start(raw[:], src.rearrange("(p j) w -> p j w", j=PACK))
+            return raw
+
+        nc.sync.dma_start(offsets[:], offs)
+        load_words(k_words, keys_words)
+        load_bytes(nc.scalar, k_bytes, keys_scales, 0)
+        q_raw = load_rows("q_raw", query, "stage0")
+        dq_raw = load_rows("dq_raw", dquery, "stage1")
+        nc.gpsimd.dma_start(h[:], helpf)
+        load_bytes(nc.gpsimd, v_bytes, vals_scales, V_ROW)
+        load_words(v_words, vals_words)
+
+        hc = col("hc", 4)
+        for j, (scale, shift) in enumerate(((0.5, 0.0), (0.5, 1.0), (-1.0 / 16, 0.0), (1.0 / 16, 0.0))):
+            nc.gpsimd.tensor_scalar(hc[:, j : j + 1], h[:], scale, shift, ALU.mult, ALU.add)
+
+        def gather(name, pool, dtype, tag):
+            got = sb.tile([P, I], dtype, name=name, tag=tag, align_bytes=64)
+            nc.vector.tensor_copy(got[:], pool[:].indirect(offsets[:]))
+            return got
+
+        def quantise(name, raw):
+            woven = sb.tile([P, Q, PACK], BF16, name=name + "_woven", tag=name + "_woven", align_bytes=64)
+            nc.scalar.activation(
+                woven[:].rearrange("p (c i) t -> p c t i", i=4), raw[:].rearrange("p t (c i) -> p c t i", i=4), ACT.Copy
+            )
+            codes = sb.tile([P, Q], U32, name=name + "_codes", align_bytes=64)
+            scales = sb.tile([P, Q], U8, name=name + "_scales", align_bytes=64)
+            nc.vector.quantize_mx(codes[:].bitcast(FP8X4), scales[:], woven[:].rearrange("p w t -> p (w t)"))
+            return codes, scales
+
+        def product(name, rows, words, scale_rows):
+            acc = ps.tile([P, I], F32, name=name)
+            nc.tensor.matmul_mx(acc[:], lhsT=rows[0][:].bitcast(FP8X4), lhsT_scale=rows[1][:], rhs=words[:].bitcast(FP8X4), rhs_scale=scale_rows, start=True, stop=True)
+            return acc
+
+        kg_bytes = gather("kg_bytes", k_bytes, U8, "kg_bytes")
+        kg_words = gather("kg_words", k_words, U32, "kg_words")
+        q_mx = quantise("q", q_raw)
+        a = product("a", q_mx, kg_words, kg_bytes[:])
+        dq_mx = quantise("dq", dq_raw)
+        ta = product("ta", dq_mx, kg_words, kg_bytes[:])
+
+        g_raw = load_rows("g_raw", gout, "stage0")
+        base_sb = sb.tile([P, T], F32, name="base_sb", tag="stage1", align_bytes=64)
+        nc.sync.dma_start(base_sb[:], base)
+
+        a_sb = wide("a_sb")
+        nc.scalar.copy(a_sb[:], a[:])
+        vg_bytes = gather("vg_bytes", v_bytes, U8, "dq_woven")
+
+        sum_a = col("sum_a", G)
+        sum_t = col("sum_t", G)
+        nc.vector.tensor_reduce(sum_a[:], paged(a[:]), AX.X, ALU.add)
+        th = col("th", G)
+        nc.scalar.activation(th[:], sum_a[:], ACT.Tanh, scale=0.125)
+        pg = col("pg", 3 * G)
+        u, hw, nv = pg[:, 0:G], pg[:, G : 2 * G], pg[:, 2 * G : 3 * G]
+        nc.scalar.activation(u, th[:], ACT.Identity, scale=hc[:, 0:1], bias=hc[:, 1:2])
+        sq = col("sq", G)
+        nc.scalar.activation(sq[:], th[:], ACT.Square)
+        nc.scalar.activation(hw, sq[:], ACT.Identity, scale=hc[:, 2:3], bias=hc[:, 3:4])
+        nc.vector.tensor_reduce(sum_t[:], paged(ta[:]), AX.X, ALU.add)
+
+        s = wide("s")
+        nc.vector.tensor_tensor(paged(s[:]), paged(a[:]), spread(u), ALU.mult)
+        nc.vector.scalar_tensor_tensor(nv, sum_t[:], -1.0, hw, ALU.mult, ALU.mult)
+        nmax = col("nmax")
+        nc.vector.tensor_reduce(nmax[:], s[:], AX.X, ALU.max, negate=True)
+        nk = col("nk", G)
+        nc.vector.scalar_tensor_tensor(nk[:], sum_t[:], 0.25, th[:], ALU.mult, ALU.mult)
+        p = wide("p")
+        z = col("z")
+        nc.scalar.activation(p[:], s[:], ACT.Exp, bias=nmax[:], accum_out=z[:])
+        pgm = col("pgm", 3 * G)
+        um, hm, vm = pgm[:, 0:G], pgm[:, G : 2 * G], pgm[:, 2 * G : 3 * G]
+        nc.gpsimd.tensor_scalar(pgm[:], pg[:], -512.0, 0.0, ALU.mult, ALU.add)
+
+        vg_words = gather("vg_words", v_words, U32, "vg_words")
+        g_mx = quantise("g", g_raw)
+        c = product("c", g_mx, vg_words, vg_bytes[V_ROW:P, :])
+
+        rz = col("rz")
+        nc.vector.reciprocal(rz[:], z[:])
+        pn = wide("pn")
+        nc.scalar.activation(pn[:], p[:], ACT.Copy, scale=rz[:])
+        nva = wide("nva")
+        by_page(nva, a_sb, nv)
+        tu = wide("tu")
+        nc.vector.tensor_tensor(paged(tu[:]), paged(ta[:]), spread(u), ALU.mult)
+
+        pc = wide("pc")
+        cbar = col("cbar")
+        nc.vector.scalar_tensor_tensor(pc[:], c[:], rz[:], p[:], ALU.mult, ALU.mult, accum_out=cbar[:])
+        ts = wide("ts")
+        nc.vector.tensor_tensor(ts[:], tu[:], nva[:], ALU.subtract)
+        ds = wide("ds")
+        nc.vector.scalar_tensor_tensor(ds[:], c[:], cbar[:], pn[:], ALU.subtract, ALU.mult)
+        pts = wide("pts")
+        tbar = col("tbar")
+        nc.vector.scalar_tensor_tensor(pts[:], ts[:], 1.0, pn[:], ALU.mult, ALU.mult, accum_out=tbar[:])
+        nka = wide("nka")
+        by_page(nka, a_sb, nk)
+        vds = wide("vds")
+        by_page(vds, ds, vm)
+        w = wide("w")
+        cov = col("cov")
+        nc.vector.scalar_tensor_tensor(w[:], ts[:], tbar[:], ds[:], ALU.subtract, ALU.mult, accum_out=cov[:])
+        nt = wide("nt")
+        nc.vector.tensor_tensor(nt[:], nka[:], ta[:], ALU.subtract)
+        ntds = wide("ntds")
+        nc.vector.scalar_tensor_tensor(ntds[:], pn[:], cov[:], w[:], ALU.mult, ALU.subtract)
+        zz = sb.tile([P, 2, I], F32, name="zz", align_bytes=64)
+        nc.vector.tensor_tensor(zz[:, 0, :], nt[:], ds[:], ALU.mult)
+        nc.vector.tensor_tensor(zz[:, 1, :], a[:], ntds[:], ALU.mult)
+        x1 = wide("x1")
+        by_page(x1, ntds, um)
+        ns = col("ns", G)
+        nc.vector.tensor_reduce(ns[:], zz[:].rearrange("p t (g j) -> p g t j", j=PAGE), AX.XY, ALU.add)
+        te = col("te", G)
+        nc.vector.tensor_tensor(te[:], ns[:], hm, ALU.mult)
+        x2 = wide("x2")
+        nc.vector.tensor_tensor(paged(x2[:]), paged(vds[:]), spread(te[:]), ALU.add)
+        nc.vector.tensor_tensor(window[:].indirect(offsets[:]), x1[:], x2[:], ALU.add)
+
+        width = T // CHUNKS
+        for n in range(CHUNKS):
+            cols = slice(n * width, (n + 1) * width)
+            res = sb.tile([P, width], F32, name="res%d" % n, align_bytes=64)
+            nc.vector.tensor_tensor(res[:], window[:, cols], base_sb[:, cols], ALU.add)
+            nc.sync.dma_start(out[:, cols], res[:])

@@ -20,7 +20,7 @@ P = 128
 PACK = 4
 PAGE = I // G
 V_ROW = 4
-CHUNKS = 4
+CHUNKS = 8
 
 
 def tile_attend_hvpagemates_s_kernel(tc, query, keys_words, keys_scales, helpf, gout, vals_words, vals_scales, dquery, base, offs, out):
@@ -39,7 +39,7 @@ def tile_attend_hvpagemates_s_kernel(tc, query, keys_words, keys_scales, helpf, 
             return ap.rearrange("p (g j) -> p g j", j=PAGE)
 
         def spread(ap):
-            return ap.unsqueeze(2).to_broadcast([P, G, PAGE])
+            return ap.unsqueeze(2).to_broadcast([P, ap.shape[1], PAGE])
 
         def by_page(dst, src, factor):
             for g in range(G):
@@ -48,21 +48,20 @@ def tile_attend_hvpagemates_s_kernel(tc, query, keys_words, keys_scales, helpf, 
 
         offsets = sb.tile([P, I // 16], U16, name="offsets")
         k_words = sb.tile([P, T], U32, name="k_words", align_bytes=64)
-        v_words = sb.tile([P, T], U32, name="v_words", align_bytes=64)
         k_bytes = sb.tile([P, T], U8, name="k_bytes", align_bytes=64)
         v_bytes = sb.tile([P, T], U8, name="v_bytes", align_bytes=64)
         window = sb.tile([P, T], F32, name="window", align_bytes=64)
         h = col("h")
 
-        nc.vector.memset(k_bytes[:].bitcast(I32), 0)
-        nc.vector.memset(v_bytes[:].bitcast(I32), 0)
+        nc.gpsimd.memset(k_bytes[:].bitcast(I32), 0)
+        nc.gpsimd.memset(v_bytes[:].bitcast(I32), 0)
         nc.vector.memset(window[:], 0.0)
 
         def load_words(dst, src):
             nc.sync.dma_start(dst[:].bitcast(I32), src[0].rearrange("p n t -> p (n t)").bitcast(I32))
 
-        def load_bytes(queue, dst, src, row):
-            for quad in range(4):
+        def load_bytes(queues, dst, src, row):
+            for quad, queue in enumerate(queues):
                 queue.dma_start(dst[32 * quad + row : 32 * quad + row + 4, :].bitcast(I32), src[0, 4 * quad : 4 * quad + 4, :].bitcast(I32))
 
         def load_rows(name, src, tag):
@@ -71,13 +70,12 @@ def tile_attend_hvpagemates_s_kernel(tc, query, keys_words, keys_scales, helpf, 
             return raw
 
         nc.sync.dma_start(offsets[:], offs)
-        load_words(k_words, keys_words)
-        load_bytes(nc.scalar, k_bytes, keys_scales, 0)
-        q_raw = load_rows("q_raw", query, "stage0")
-        dq_raw = load_rows("dq_raw", dquery, "stage1")
+        load_bytes([nc.sync] * 4, k_bytes, keys_scales, 0)
         nc.gpsimd.dma_start(h[:], helpf)
-        load_bytes(nc.gpsimd, v_bytes, vals_scales, V_ROW)
-        load_words(v_words, vals_words)
+        q_raw = load_rows("q_raw", query, "stage0")
+        load_words(k_words, keys_words)
+        dq_raw = load_rows("dq_raw", dquery, "late")
+        load_bytes([nc.sync] * 4, v_bytes, vals_scales, V_ROW)
 
         hc = col("hc", 4)
         for j, (scale, shift) in enumerate(((0.5, 0.0), (0.5, 1.0), (-1.0 / 16, 0.0), (1.0 / 16, 0.0))):
@@ -88,39 +86,48 @@ def tile_attend_hvpagemates_s_kernel(tc, query, keys_words, keys_scales, helpf, 
             nc.vector.tensor_copy(got[:], pool[:].indirect(offsets[:]))
             return got
 
-        def quantise(name, raw):
-            woven = sb.tile([P, Q, PACK], BF16, name=name + "_woven", tag=name + "_woven", align_bytes=64)
-            nc.scalar.activation(
-                woven[:].rearrange("p (c i) t -> p c t i", i=4), raw[:].rearrange("p t (c i) -> p c t i", i=4), ACT.Copy
-            )
-            codes = sb.tile([P, Q], U32, name=name + "_codes", align_bytes=64)
-            scales = sb.tile([P, Q], U8, name=name + "_scales", align_bytes=64)
+        def quantise(name, raws):
+            width = len(raws) * Q
+            woven = sb.tile([P, width, PACK], BF16, name=name + "_woven", align_bytes=64)
+            for n, raw in enumerate(raws):
+                nc.scalar.activation(
+                    woven[:, n * Q : (n + 1) * Q, :].rearrange("p (c i) t -> p c t i", i=4),
+                    raw[:].rearrange("p t (c i) -> p c t i", i=4),
+                    ACT.Copy,
+                )
+            codes = sb.tile([P, width], U32, name=name + "_codes", align_bytes=64)
+            scales = sb.tile([P, width], U8, name=name + "_scales", align_bytes=64)
             nc.vector.quantize_mx(codes[:].bitcast(FP8X4), scales[:], woven[:].rearrange("p w t -> p (w t)"))
-            return codes, scales
+            return [(codes[:, n * Q : (n + 1) * Q], scales[:, n * Q : (n + 1) * Q]) for n in range(len(raws))]
 
         def product(name, rows, words, scale_rows):
-            acc = ps.tile([P, I], F32, name=name)
-            nc.tensor.matmul_mx(acc[:], lhsT=rows[0][:].bitcast(FP8X4), lhsT_scale=rows[1][:], rhs=words[:].bitcast(FP8X4), rhs_scale=scale_rows, start=True, stop=True)
+            acc = ps.tile([P, words.shape[1]], F32, name=name)
+            nc.tensor.matmul_mx(acc[:], lhsT=rows[0].bitcast(FP8X4), lhsT_scale=rows[1], rhs=words.bitcast(FP8X4), rhs_scale=scale_rows, start=True, stop=True)
             return acc
 
-        kg_bytes = gather("kg_bytes", k_bytes, U8, "kg_bytes")
-        kg_words = gather("kg_words", k_words, U32, "kg_words")
-        q_mx = quantise("q", q_raw)
-        a = product("a", q_mx, kg_words, kg_bytes[:])
-        dq_mx = quantise("dq", dq_raw)
-        ta = product("ta", dq_mx, kg_words, kg_bytes[:])
+        slots = [slice(n * I // 2, (n + 1) * I // 2) for n in range(2)]
+        pages = [slice(n * G // 2, (n + 1) * G // 2) for n in range(2)]
+        lists = [slice(n * I // 32, (n + 1) * I // 32) for n in range(2)]
 
+        kg_bytes = gather("kg_bytes", k_bytes, U8, "kg_bytes")
+        q_mx, dq_mx = quantise("q", [q_raw, dq_raw])
         g_raw = load_rows("g_raw", gout, "stage0")
-        base_sb = sb.tile([P, T], F32, name="base_sb", tag="stage1", align_bytes=64)
-        nc.sync.dma_start(base_sb[:], base)
+        v_words = sb.tile([P, T], U32, name="v_words", tag="late", align_bytes=64)
+        load_words(v_words, vals_words)
+        (g_mx,) = quantise("g", [g_raw])
+        kg_words = sb.tile([P, I], U32, name="kg_words", align_bytes=64)
+        a = []
+        for n in range(2):
+            nc.vector.tensor_copy(kg_words[:, slots[n]], k_words[:].indirect(offsets[:, lists[n]]))
+            a.append(product("a%d" % n, q_mx, kg_words[:, slots[n]], kg_bytes[:, slots[n]]))
+        ta = product("ta", dq_mx, kg_words[:], kg_bytes[:])
 
         a_sb = wide("a_sb")
-        nc.scalar.copy(a_sb[:], a[:])
-        vg_bytes = gather("vg_bytes", v_bytes, U8, "dq_woven")
-
-        sum_a = col("sum_a", G)
+        sum_a = sb.tile([P, G], F32, name="sum_a", tag="sum_a", align_bytes=64)
         sum_t = col("sum_t", G)
-        nc.vector.tensor_reduce(sum_a[:], paged(a[:]), AX.X, ALU.add)
+        for n in range(2):
+            nc.vector.tensor_reduce(sum_a[:, pages[n]], paged(a[n][:]), AX.X, ALU.add)
+        nc.scalar.copy(a_sb[:, slots[0]], a[0][:])
         th = col("th", G)
         nc.scalar.activation(th[:], sum_a[:], ACT.Tanh, scale=0.125)
         pg = col("pg", 3 * G)
@@ -128,16 +135,23 @@ def tile_attend_hvpagemates_s_kernel(tc, query, keys_words, keys_scales, helpf, 
         nc.scalar.activation(u, th[:], ACT.Identity, scale=hc[:, 0:1], bias=hc[:, 1:2])
         sq = col("sq", G)
         nc.scalar.activation(sq[:], th[:], ACT.Square)
+        nc.scalar.copy(a_sb[:, slots[1]], a[1][:])
         nc.scalar.activation(hw, sq[:], ACT.Identity, scale=hc[:, 2:3], bias=hc[:, 3:4])
         nc.vector.tensor_reduce(sum_t[:], paged(ta[:]), AX.X, ALU.add)
+        sum_th = col("sum_th", G)
+        nc.vector.tensor_scalar(sum_th[:], sum_t[:], hc[:, 3:4], None, ALU.mult)
 
-        s = wide("s")
-        nc.vector.tensor_tensor(paged(s[:]), paged(a[:]), spread(u), ALU.mult)
-        nc.vector.scalar_tensor_tensor(nv, sum_t[:], -1.0, hw, ALU.mult, ALU.mult)
-        nmax = col("nmax")
-        nc.vector.tensor_reduce(nmax[:], s[:], AX.X, ALU.max, negate=True)
+        nc.vector.scalar_tensor_tensor(nv, sq[:], 1.0, sum_th[:], ALU.subtract, ALU.mult)
         nk = col("nk", G)
         nc.vector.scalar_tensor_tensor(nk[:], sum_t[:], 0.25, th[:], ALU.mult, ALU.mult)
+        nva = wide("nva")
+        nc.gpsimd.tensor_tensor(paged(nva[:]), paged(a_sb[:]), spread(nv), ALU.mult)
+        vg_bytes = gather("vg_bytes", v_bytes, U8, "sum_a")
+        s = sb.tile([P, I], F32, name="s", tag="s", align_bytes=64)
+        for n in range(2):
+            nc.vector.tensor_tensor(paged(s[:, slots[n]]), paged(a[n][:]), spread(u[:, pages[n]]), ALU.mult)
+        nmax = col("nmax")
+        nc.vector.tensor_reduce(nmax[:], s[:], AX.X, ALU.max, negate=True)
         p = wide("p")
         z = col("z")
         nc.scalar.activation(p[:], s[:], ACT.Exp, bias=nmax[:], accum_out=z[:])
@@ -146,50 +160,56 @@ def tile_attend_hvpagemates_s_kernel(tc, query, keys_words, keys_scales, helpf, 
         nc.gpsimd.tensor_scalar(pgm[:], pg[:], -512.0, 0.0, ALU.mult, ALU.add)
 
         vg_words = gather("vg_words", v_words, U32, "vg_words")
-        g_mx = quantise("g", g_raw)
-        c = product("c", g_mx, vg_words, vg_bytes[V_ROW:P, :])
+        base_sb = sb.tile([P, T], F32, name="base_sb", tag="s", align_bytes=64)
+        nc.sync.dma_start(base_sb[:], base)
+        c = product("c", g_mx, vg_words[:], vg_bytes[V_ROW:P, :])
 
-        rz = col("rz")
+        rz = sb.tile([P, 1], F32, name="rz", tag="late", align_bytes=64)
         nc.vector.reciprocal(rz[:], z[:])
         pn = wide("pn")
         nc.scalar.activation(pn[:], p[:], ACT.Copy, scale=rz[:])
-        nva = wide("nva")
-        by_page(nva, a_sb, nv)
         tu = wide("tu")
         nc.vector.tensor_tensor(paged(tu[:]), paged(ta[:]), spread(u), ALU.mult)
 
+        nka = wide("nka")
+        by_page(nka, a_sb, nk)
+        ts = wide("ts")
+        nc.vector.tensor_tensor(ts[:], tu[:], nva[:], ALU.subtract)
         pc = wide("pc")
         cbar = col("cbar")
         nc.vector.scalar_tensor_tensor(pc[:], c[:], rz[:], p[:], ALU.mult, ALU.mult, accum_out=cbar[:])
-        ts = wide("ts")
-        nc.vector.tensor_tensor(ts[:], tu[:], nva[:], ALU.subtract)
-        ds = wide("ds")
-        nc.vector.scalar_tensor_tensor(ds[:], c[:], cbar[:], pn[:], ALU.subtract, ALU.mult)
         pts = wide("pts")
         tbar = col("tbar")
         nc.vector.scalar_tensor_tensor(pts[:], ts[:], 1.0, pn[:], ALU.mult, ALU.mult, accum_out=tbar[:])
-        nka = wide("nka")
-        by_page(nka, a_sb, nk)
+        ds = wide("ds")
+        nc.vector.scalar_tensor_tensor(ds[:], c[:], cbar[:], pn[:], ALU.subtract, ALU.mult)
         vds = wide("vds")
         by_page(vds, ds, vm)
+        nt = wide("nt")
+        nc.vector.tensor_tensor(nt[:], nka[:], ta[:], ALU.subtract)
         w = wide("w")
         cov = col("cov")
         nc.vector.scalar_tensor_tensor(w[:], ts[:], tbar[:], ds[:], ALU.subtract, ALU.mult, accum_out=cov[:])
-        nt = wide("nt")
-        nc.vector.tensor_tensor(nt[:], nka[:], ta[:], ALU.subtract)
         ntds = wide("ntds")
         nc.vector.scalar_tensor_tensor(ntds[:], pn[:], cov[:], w[:], ALU.mult, ALU.subtract)
-        zz = sb.tile([P, 2, I], F32, name="zz", align_bytes=64)
-        nc.vector.tensor_tensor(zz[:, 0, :], nt[:], ds[:], ALU.mult)
-        nc.vector.tensor_tensor(zz[:, 1, :], a[:], ntds[:], ALU.mult)
         x1 = wide("x1")
         by_page(x1, ntds, um)
-        ns = col("ns", G)
-        nc.vector.tensor_reduce(ns[:], zz[:].rearrange("p t (g j) -> p g t j", j=PAGE), AX.XY, ALU.add)
-        te = col("te", G)
-        nc.vector.tensor_tensor(te[:], ns[:], hm, ALU.mult)
         x2 = wide("x2")
-        nc.vector.tensor_tensor(paged(x2[:]), paged(vds[:]), spread(te[:]), ALU.add)
+        zz = [sb.tile([P, 2, I // 2], F32, name="zz%d" % n, align_bytes=64) for n in range(2)]
+        ns = [col("ns%d" % n, G // 2) for n in range(2)]
+        te = [col("te%d" % n, G // 2) for n in range(2)]
+        for n in range(2):
+            nc.vector.tensor_tensor(zz[n][:, 0, :], nt[:, slots[n]], ds[:, slots[n]], ALU.mult)
+        for n in range(2):
+            nc.vector.tensor_tensor(zz[n][:, 1, :], a[n][:], ntds[:, slots[n]], ALU.mult)
+        for n in range(2):
+            nc.vector.tensor_reduce(ns[n][:], zz[n][:].rearrange("p t (g j) -> p g t j", j=PAGE), AX.XY, ALU.add)
+        for n in range(2):
+            nc.vector.tensor_tensor(te[n][:], ns[n][:], hm[:, pages[n]], ALU.mult)
+        for n in range(2):
+            nc.vector.tensor_tensor(
+                paged(x2[:, slots[n]]), paged(vds[:, slots[n]]), spread(te[n][:]), ALU.add
+            )
         nc.vector.tensor_tensor(window[:].indirect(offsets[:]), x1[:], x2[:], ALU.add)
 
         width = T // CHUNKS

@@ -20,7 +20,7 @@ P = 128
 PACK = 4
 PAGE = I // G
 V_ROW = 4
-CHUNKS = 8
+CHUNKS = (256, 512, 512, 512, 256)
 
 
 def tile_attend_hvpagemates_s_kernel(tc, query, keys_words, keys_scales, helpf, gout, vals_words, vals_scales, dquery, base, offs, out):
@@ -54,7 +54,7 @@ def tile_attend_hvpagemates_s_kernel(tc, query, keys_words, keys_scales, helpf, 
         h = col("h")
 
         nc.gpsimd.memset(k_bytes[:].bitcast(I32), 0)
-        nc.gpsimd.memset(v_bytes[:].bitcast(I32), 0)
+        nc.vector.memset(v_bytes[:].bitcast(I32), 0)
         nc.vector.memset(window[:], 0.0)
 
         def load_words(dst, src):
@@ -70,12 +70,12 @@ def tile_attend_hvpagemates_s_kernel(tc, query, keys_words, keys_scales, helpf, 
             return raw
 
         nc.sync.dma_start(offsets[:], offs)
-        load_bytes([nc.sync] * 4, k_bytes, keys_scales, 0)
+        load_bytes([nc.scalar] * 4, k_bytes, keys_scales, 0)
         nc.gpsimd.dma_start(h[:], helpf)
         q_raw = load_rows("q_raw", query, "stage0")
-        load_words(k_words, keys_words)
         dq_raw = load_rows("dq_raw", dquery, "late")
-        load_bytes([nc.sync] * 4, v_bytes, vals_scales, V_ROW)
+        load_words(k_words, keys_words)
+        load_bytes([nc.gpsimd] * 4, v_bytes, vals_scales, V_ROW)
 
         hc = col("hc", 4)
         for j, (scale, shift) in enumerate(((0.5, 0.0), (0.5, 1.0), (-1.0 / 16, 0.0), (1.0 / 16, 0.0))):
@@ -212,9 +212,8 @@ def tile_attend_hvpagemates_s_kernel(tc, query, keys_words, keys_scales, helpf, 
             )
         nc.vector.tensor_tensor(window[:].indirect(offsets[:]), x1[:], x2[:], ALU.add)
 
-        width = T // CHUNKS
-        for n in range(CHUNKS):
-            cols = slice(n * width, (n + 1) * width)
+        for n, width in enumerate(CHUNKS):
+            cols = slice(sum(CHUNKS[:n]), sum(CHUNKS[: n + 1]))
             res = sb.tile([P, width], F32, name="res%d" % n, align_bytes=64)
             nc.vector.tensor_tensor(res[:], window[:, cols], base_sb[:, cols], ALU.add)
             nc.sync.dma_start(out[:, cols], res[:])

@@ -193,7 +193,7 @@ def tile_attend_hvpagemates_s_kernel(tc, query, keys_words, keys_scales, helpf, 
         ntds = wide("ntds")
         nc.vector.scalar_tensor_tensor(ntds[:], pn[:], cov[:], w[:], ALU.mult, ALU.subtract)
         x1 = wide("x1")
-        by_page(x1, ntds, um)
+        nc.gpsimd.tensor_tensor(paged(x1[:]), paged(ntds[:]), spread(um), ALU.mult)
         x2 = wide("x2")
         zz = [sb.tile([P, 2, I // 2], F32, name="zz%d" % n, align_bytes=64) for n in range(2)]
         ns = [col("ns%d" % n, G // 2) for n in range(2)]

from contextlib import ExitStack

import concourse.mybir as mybir

D, E, T, I, Q, G = 512, 512, 2048, 512, 128, 32
FLOPS = 3 * 2 * 512 * 512 * 128

F32 = mybir.dt.float32
BF16 = mybir.dt.bfloat16
I32 = mybir.dt.int32
U32 = mybir.dt.uint32
U16 = mybir.dt.uint16
U8 = mybir.dt.uint8
FP8X4 = mybir.dt.float8_e4m3fn_x4
ALU = mybir.AluOpType
ACT = mybir.ActivationFunctionType
AX = mybir.AxisListType

P = 128
PACK = 4
PAGE = I // G
V_ROW = 4
CHUNKS = (256, 512, 512, 512, 256)


def tile_attend_hvpagemates_s_kernel(tc, query, keys_words, keys_scales, helpf, gout, vals_words, vals_scales, dquery, base, offs, out):
    nc = tc.nc
    with ExitStack() as ctx:
        sb = ctx.enter_context(tc.tile_pool(name="sb", bufs=1))
        ps = ctx.enter_context(tc.psum_pool(name="ps", bufs=1))

        def wide(name):
            return sb.tile([P, I], F32, name=name, align_bytes=64)

        def col(name, n=1):
            return sb.tile([P, n], F32, name=name)

        def paged(ap):
            return ap.rearrange("p (g j) -> p g j", j=PAGE)

        def spread(ap):
            return ap.unsqueeze(2).to_broadcast([P, ap.shape[1], PAGE])

        def by_page(dst, src, factor):
            for g in range(G):
                cols = slice(g * PAGE, (g + 1) * PAGE)
                nc.scalar.activation(dst[:, cols], src[:, cols], ACT.Copy, scale=factor[:, g : g + 1])

        offsets = sb.tile([P, I // 16], U16, name="offsets")
        k_words = sb.tile([P, T], U32, name="k_words", align_bytes=64)
        k_bytes = sb.tile([P, T], U8, name="k_bytes", align_bytes=64)
        v_bytes = sb.tile([P, T], U8, name="v_bytes", align_bytes=64)
        window = sb.tile([P, T], F32, name="window", align_bytes=64)
        h = col("h")

        nc.gpsimd.memset(k_bytes[:].bitcast(I32), 0)
        nc.vector.memset(v_bytes[:].bitcast(I32), 0)
        nc.vector.memset(window[:], 0.0)

        def load_words(dst, src):
            nc.sync.dma_start(dst[:].bitcast(I32), src[0].rearrange("p n t -> p (n t)").bitcast(I32))

        def load_bytes(queues, dst, src, row):
            for quad, queue in enumerate(queues):
                queue.dma_start(dst[32 * quad + row : 32 * quad + row + 4, :].bitcast(I32), src[0, 4 * quad : 4 * quad + 4, :].bitcast(I32))

        def load_rows(name, src, tag):
            raw = sb.tile([P, PACK, Q], F32, name=name, tag=tag, align_bytes=64)
            nc.sync.dma_start(raw[:], src.rearrange("(p j) w -> p j w", j=PACK))
            return raw

        nc.sync.dma_start(offsets[:], offs)
        load_bytes([nc.scalar] * 4, k_bytes, keys_scales, 0)
        nc.gpsimd.dma_start(h[:], helpf)
        q_raw = load_rows("q_raw", query, "stage0")
        dq_raw = load_rows("dq_raw", dquery, "late")
        load_words(k_words, keys_words)
        load_bytes([nc.gpsimd] * 4, v_bytes, vals_scales, V_ROW)

        hc = col("hc", 4)
        for j, (scale, shift) in enumerate(((0.5, 0.0), (0.5, 1.0), (-1.0 / 16, 0.0), (1.0 / 16, 0.0))):
            nc.gpsimd.tensor_scalar(hc[:, j : j + 1], h[:], scale, shift, ALU.mult, ALU.add)

        def gather(name, pool, dtype, tag):
            got = sb.tile([P, I], dtype, name=name, tag=tag, align_bytes=64)
            nc.vector.tensor_copy(got[:], pool[:].indirect(offsets[:]))
            return got

        def quantise(name, raws):
            width = len(raws) * Q
            woven = sb.tile([P, width, PACK], BF16, name=name + "_woven", align_bytes=64)
            for n, raw in enumerate(raws):
                nc.scalar.activation(
                    woven[:, n * Q : (n + 1) * Q, :].rearrange("p (c i) t -> p c t i", i=4),
                    raw[:].rearrange("p t (c i) -> p c t i", i=4),
                    ACT.Copy,
                )
            codes = sb.tile([P, width], U32, name=name + "_codes", align_bytes=64)
            scales = sb.tile([P, width], U8, name=name + "_scales", align_bytes=64)
            nc.vector.quantize_mx(codes[:].bitcast(FP8X4), scales[:], woven[:].rearrange("p w t -> p (w t)"))
            return [(codes[:, n * Q : (n + 1) * Q], scales[:, n * Q : (n + 1) * Q]) for n in range(len(raws))]

        def product(name, rows, words, scale_rows):
            acc = ps.tile([P, words.shape[1]], F32, name=name)
            nc.tensor.matmul_mx(acc[:], lhsT=rows[0].bitcast(FP8X4), lhsT_scale=rows[1], rhs=words.bitcast(FP8X4), rhs_scale=scale_rows, start=True, stop=True)
            return acc

        slots = [slice(n * I // 2, (n + 1) * I // 2) for n in range(2)]
        pages = [slice(n * G // 2, (n + 1) * G // 2) for n in range(2)]
        lists = [slice(n * I // 32, (n + 1) * I // 32) for n in range(2)]

        kg_bytes = gather("kg_bytes", k_bytes, U8, "kg_bytes")
        q_mx, dq_mx = quantise("q", [q_raw, dq_raw])
        g_raw = load_rows("g_raw", gout, "stage0")
        v_words = sb.tile([P, T], U32, name="v_words", tag="late", align_bytes=64)
        load_words(v_words, vals_words)
        (g_mx,) = quantise("g", [g_raw])
        kg_words = sb.tile([P, I], U32, name="kg_words", align_bytes=64)
        a = []
        for n in range(2):
            nc.vector.tensor_copy(kg_words[:, slots[n]], k_words[:].indirect(offsets[:, lists[n]]))
            a.append(product("a%d" % n, q_mx, kg_words[:, slots[n]], kg_bytes[:, slots[n]]))
        ta = product("ta", dq_mx, kg_words[:], kg_bytes[:])

        a_sb = wide("a_sb")
        sum_a = sb.tile([P, G], F32, name="sum_a", tag="sum_a", align_bytes=64)
        sum_t = col("sum_t", G)
        for n in range(2):
            nc.vector.tensor_reduce(sum_a[:, pages[n]], paged(a[n][:]), AX.X, ALU.add)
        nc.scalar.copy(a_sb[:, slots[0]], a[0][:])
        th = col("th", G)
        nc.scalar.activation(th[:], sum_a[:], ACT.Tanh, scale=0.125)
        pg = col("pg", 3 * G)
        u, hw, nv = pg[:, 0:G], pg[:, G : 2 * G], pg[:, 2 * G : 3 * G]
        nc.scalar.activation(u, th[:], ACT.Identity, scale=hc[:, 0:1], bias=hc[:, 1:2])
        sq = col("sq", G)
        nc.scalar.activation(sq[:], th[:], ACT.Square)
        nc.scalar.copy(a_sb[:, slots[1]], a[1][:])
        nc.scalar.activation(hw, sq[:], ACT.Identity, scale=hc[:, 2:3], bias=hc[:, 3:4])
        nc.vector.tensor_reduce(sum_t[:], paged(ta[:]), AX.X, ALU.add)
        sum_th = col("sum_th", G)
        nc.vector.tensor_scalar(sum_th[:], sum_t[:], hc[:, 3:4], None, ALU.mult)

        nc.vector.scalar_tensor_tensor(nv, sq[:], 1.0, sum_th[:], ALU.subtract, ALU.mult)
        nk = col("nk", G)
        nc.vector.scalar_tensor_tensor(nk[:], sum_t[:], 0.25, th[:], ALU.mult, ALU.mult)
        nva = wide("nva")
        nc.gpsimd.tensor_tensor(paged(nva[:]), paged(a_sb[:]), spread(nv), ALU.mult)
        vg_bytes = gather("vg_bytes", v_bytes, U8, "sum_a")
        s = sb.tile([P, I], F32, name="s", tag="s", align_bytes=64)
        for n in range(2):
            nc.vector.tensor_tensor(paged(s[:, slots[n]]), paged(a[n][:]), spread(u[:, pages[n]]), ALU.mult)
        nmax = col("nmax")
        nc.vector.tensor_reduce(nmax[:], s[:], AX.X, ALU.max, negate=True)
        p = wide("p")
        z = col("z")
        nc.scalar.activation(p[:], s[:], ACT.Exp, bias=nmax[:], accum_out=z[:])
        pgm = col("pgm", 3 * G)
        um, hm, vm = pgm[:, 0:G], pgm[:, G : 2 * G], pgm[:, 2 * G : 3 * G]
        nc.gpsimd.tensor_scalar(pgm[:], pg[:], -512.0, 0.0, ALU.mult, ALU.add)

        vg_words = gather("vg_words", v_words, U32, "vg_words")
        base_sb = sb.tile([P, T], F32, name="base_sb", tag="s", align_bytes=64)
        nc.sync.dma_start(base_sb[:], base)
        c = product("c", g_mx, vg_words[:], vg_bytes[V_ROW:P, :])

        rz = sb.tile([P, 1], F32, name="rz", tag="late", align_bytes=64)
        nc.vector.reciprocal(rz[:], z[:])
        pn = wide("pn")
        nc.scalar.activation(pn[:], p[:], ACT.Copy, scale=rz[:])
        tu = wide("tu")
        nc.vector.tensor_tensor(paged(tu[:]), paged(ta[:]), spread(u), ALU.mult)

        nka = wide("nka")
        by_page(nka, a_sb, nk)
        ts = wide("ts")
        nc.vector.tensor_tensor(ts[:], tu[:], nva[:], ALU.subtract)
        pc = wide("pc")
        cbar = col("cbar")
        nc.vector.scalar_tensor_tensor(pc[:], c[:], rz[:], p[:], ALU.mult, ALU.mult, accum_out=cbar[:])
        pts = wide("pts")
        tbar = col("tbar")
        nc.vector.scalar_tensor_tensor(pts[:], ts[:], 1.0, pn[:], ALU.mult, ALU.mult, accum_out=tbar[:])
        ds = wide("ds")
        nc.vector.scalar_tensor_tensor(ds[:], c[:], cbar[:], pn[:], ALU.subtract, ALU.mult)
        vds = wide("vds")
        by_page(vds, ds, vm)
        nt = wide("nt")
        nc.vector.tensor_tensor(nt[:], nka[:], ta[:], ALU.subtract)
        w = wide("w")
        cov = col("cov")
        nc.vector.scalar_tensor_tensor(w[:], ts[:], tbar[:], ds[:], ALU.subtract, ALU.mult, accum_out=cov[:])
        ntds = wide("ntds")
        nc.vector.scalar_tensor_tensor(ntds[:], pn[:], cov[:], w[:], ALU.mult, ALU.subtract)
        x1 = wide("x1")
        nc.gpsimd.tensor_tensor(paged(x1[:]), paged(ntds[:]), spread(um), ALU.mult)
        x2 = wide("x2")
        zz = [sb.tile([P, 2, I // 2], F32, name="zz%d" % n, align_bytes=64) for n in range(2)]
        ns = [col("ns%d" % n, G // 2) for n in range(2)]
        te = [col("te%d" % n, G // 2) for n in range(2)]
        for n in range(2):
            nc.vector.tensor_tensor(zz[n][:, 0, :], nt[:, slots[n]], ds[:, slots[n]], ALU.mult)
        for n in range(2):
            nc.vector.tensor_tensor(zz[n][:, 1, :], a[n][:], ntds[:, slots[n]], ALU.mult)
        for n in range(2):
            nc.vector.tensor_reduce(ns[n][:], zz[n][:].rearrange("p t (g j) -> p g t j", j=PAGE), AX.XY, ALU.add)
        for n in range(2):
            nc.vector.tensor_tensor(te[n][:], ns[n][:], hm[:, pages[n]], ALU.mult)
        for n in range(2):
            nc.vector.tensor_tensor(
                paged(x2[:, slots[n]]), paged(vds[:, slots[n]]), spread(te[n][:]), ALU.add
            )
        nc.vector.tensor_tensor(window[:].indirect(offsets[:]), x1[:], x2[:], ALU.add)

        for n, width in enumerate(CHUNKS):
            cols = slice(sum(CHUNKS[:n]), sum(CHUNKS[: n + 1]))
            res = sb.tile([P, width], F32, name="res%d" % n, align_bytes=64)
            nc.vector.tensor_tensor(res[:], window[:, cols], base_sb[:, cols], ALU.add)
            nc.sync.dma_start(out[:, cols], res[:])
